import numpy as np
import ml_dtypes


def mxq(x, axis, fmt="e4m3"):
    dtype, down = {"e4m3": (ml_dtypes.float8_e4m3fn, 7), "e5m2": (ml_dtypes.float8_e5m2, 14)}[fmt]
    v = np.moveaxis(np.asarray(x, np.float32).astype(ml_dtypes.bfloat16).astype(np.float64), axis, -1)
    blocks = v.reshape(v.shape[:-1] + (-1, 32))
    amax = np.abs(blocks).max(-1, keepdims=True)
    byte = np.maximum(np.where(amax > 0, np.frexp(amax)[1] - 1 + 127, 0) - down, 1)
    scale = np.exp2(byte - 127.0)
    codes = (blocks / scale).astype(np.float32).astype(dtype).astype(np.float64)
    return np.moveaxis((codes * scale).reshape(v.shape), -1, axis)


WIDE = False


def mx_kscale(k):
    if not WIDE:
        return np.ones(k)
    levels = np.array([10, -10, 5, -5, 0])
    if k % 512:
        return np.exp2(np.random.permutation(np.resize(levels, k // 32))).repeat(32)
    a = np.empty((k // 512, 16))
    for p in range(k // 512):
        a[p, :8] = np.random.permutation(np.resize(levels, 8))
        for g in range(8):
            far = levels[np.abs(levels - a[p, g]) >= 10]
            a[p, g + 8] = far[np.random.randint(len(far))]
    return np.exp2(a.ravel()).repeat(32)


BF16 = ml_dtypes.bfloat16


def bf(x):
    return np.asarray(x, np.float32).astype(BF16)


def f64(x):
    return np.asarray(x).astype(np.float64)


M, S, Q, D = 1024, 1024, 2048, 512

PEAK = 1.5
SPREAD = 0.5


def setup_inputs():
    s = mx_kscale(D)
    t = mx_kscale(S)
    prof = np.exp(PEAK * np.random.standard_normal((M, S)))
    prof = prof / prof.sum(axis=1, keepdims=True)
    act = np.exp(SPREAD * np.random.standard_normal(S))
    return {"seg": bf(np.random.standard_normal((S, D)) * s),
            "probe": bf(np.random.standard_normal((D, Q)) / np.sqrt(D) / s[:, None]),
            "act": bf(act * t),
            "prof": bf(prof / t)}


def reference(seg, probe, act, prof):
    e = mxq(f64(seg), 1, "e4m3") @ mxq(f64(probe), 0, "e4m3")
    b = np.exp(e) * f64(act)[:, None]
    z = mxq(f64(prof), 1, "e4m3") @ mxq(b, 0, "e4m3")
    return 1.0 / z

@@ -1,0 +1,255 @@
+from contextlib import ExitStack
+
+import concourse.mybir as mybir
+from concourse.masks import make_identity
+
+M, S, Q, D = 1024, 1024, 2048, 512
+FLOPS = 2 * S * D * Q + 2 * M * S * Q
+
+F32 = mybir.dt.float32
+BF16 = mybir.dt.bfloat16
+U32 = mybir.dt.uint32
+U8 = mybir.dt.uint8
+FP8X4 = mybir.dt.float8_e4m3fn_x4
+ACT = mybir.ActivationFunctionType
+
+P = 128
+PACK = 4
+KP = P * PACK
+NT = 512
+NQ = Q // NT
+NG = S // KP
+NI = M // P
+
+
+def tile_cosmo_segment_activities_s7_kernel(tc, seg, probe, act, prof, out):
+    nc = tc.nc
+    with ExitStack() as ctx:
+        keep = ctx.enter_context(tc.tile_pool(name="keep", bufs=1))
+        work = ctx.enter_context(tc.tile_pool(name="work", bufs=2))
+        outp = ctx.enter_context(tc.tile_pool(name="outp", bufs=4))
+        psum = ctx.enter_context(tc.psum_pool(name="psum", bufs=8))
+
+        seg_view = seg.rearrange("(g p t) d -> g p t d", g=NG, t=PACK)
+        probe_view = probe.rearrange("(p j) q -> p j q", j=PACK)
+        prof_view = prof.rearrange("(i r) s -> r i s", r=P)
+        act_view = act.rearrange("(g p t) -> p g t", g=NG, t=PACK)
+
+        ident = keep.tile([P, P], F32, name="ident")
+        make_identity(nc, ident[:])
+
+        seg_codes = keep.tile([P, S], U32, name="seg_codes", align_bytes=64)
+        seg_scales = keep.tile([P, S], U8, name="seg_scales", align_bytes=64)
+        probe_codes = keep.tile([P, Q], U32, name="probe_codes", align_bytes=64)
+        probe_scales = keep.tile([P, Q], U8, name="probe_scales", align_bytes=64)
+        prof_codes = keep.tile([P, NI, NG, P], U32, name="prof_codes", align_bytes=64)
+        prof_scales = keep.tile([P, NI, NG, P], U8, name="prof_scales", align_bytes=64)
+        b_codes = keep.tile([P, NG, Q], U32, name="b_codes", align_bytes=64)
+        b_scales = keep.tile([P, NG, Q], U8, name="b_scales", align_bytes=64)
+
+        one = keep.tile([P, 1], F32, name="one")
+        junk = keep.tile([P, 1], F32, name="junk")
+        act_sb = keep.tile([P, NG, PACK], BF16, name="act_sb")
+        ln_act = keep.tile([P, NG * PACK], F32, name="ln_act")
+
+        def psum_bank():
+            bank = psum.tile([P, NT], F32, name="bank")
+            return bank
+
+        with tc.manual_schedule():
+            nc.scalar.dma_start(out=act_sb[:], in_=act_view)
+            nc.vector.memset(one[:], 1.0)
+            nc.scalar.activation(out=junk[:], in_=one[:], func=ACT.Ln)
+
+            seg_raw = [keep.tile([P, PACK, D], BF16, name="seg_raw%d" % g) for g in range(NG)]
+            probe_raw = [keep.tile([P, PACK, NT], BF16, name="probe_raw%d" % c) for c in range(NQ)]
+            prof_raw = [keep.tile([P, 2, S], BF16, name="prof_raw%d" % h) for h in range(NI // 2)]
+
+            def load_seg(g):
+                nc.sync.dma_start(out=seg_raw[g][:], in_=seg_view[g])
+
+            def load_probe(c):
+                nc.sync.dma_start(out=probe_raw[c][:], in_=probe_view[:, :, c * NT:(c + 1) * NT])
+
+            def load_prof(h):
+                nc.sync.dma_start(out=prof_raw[h][:], in_=prof_view[:, 2 * h:2 * h + 2, :])
+
+            load_seg(0)
+            load_probe(0)
+            load_seg(1)
+            load_probe(1)
+            load_prof(0)
+            load_probe(2)
+            load_prof(1)
+            load_probe(3)
+            load_prof(2)
+            load_prof(3)
+
+            nc.scalar.activation(out=ln_act[:], in_=act_sb[:].rearrange("p g t -> p (g t)"), func=ACT.Ln)
+            nc.scalar.activation(out=junk[:], in_=one[:], func=ACT.Exp)
+
+            seg_grouped = {}
+
+            def seg_transposes(g):
+                grouped = work.tile([P, NT * PACK], BF16, name="seg_grouped", align_bytes=64)
+                seg_grouped[g] = grouped
+                words_out = grouped[:].bitcast(F32).rearrange("j (t p u) -> j t p u", t=PACK, u=2)
+                for half in range(2):
+                    bank = psum_bank()
+                    for k in range(2):
+                        words = seg_raw[g][:, 2 * half + k, :].bitcast(F32)
+                        for u in range(2):
+                            x = 2 * k + u
+                            nc.tensor.transpose(bank[:, x * P:(x + 1) * P], words[:, u::2], ident[:])
+                    nc.scalar.copy(
+                        out=words_out[:, 2 * half:2 * half + 2],
+                        in_=bank[:].rearrange("j (t u p) -> j t p u", t=2, u=2),
+                    )
+
+            def seg_quantize(g):
+                cols = slice(g * KP, (g + 1) * KP)
+                nc.vector.quantize_mx(
+                    out=seg_codes[:, cols].bitcast(FP8X4), scales=seg_scales[:, cols], in_=seg_grouped[g][:])
+
+            probe_grouped = {}
+
+            def interleave(dst, src):
+                nc.vector.tensor_copy(
+                    out=dst.rearrange("p (c i t) -> p c t i", i=4, t=PACK),
+                    in_=src.rearrange("p t (c i) -> p c t i", i=4))
+
+            def probe_interleave(c):
+                grouped = work.tile([P, NT * PACK], BF16, name="probe_grouped", align_bytes=64)
+                probe_grouped[c] = grouped
+                interleave(grouped[:], probe_raw[c][:])
+
+            def probe_quantize(c):
+                cols = slice(c * NT, (c + 1) * NT)
+                nc.vector.quantize_mx(
+                    out=probe_codes[:, cols].bitcast(FP8X4), scales=probe_scales[:, cols], in_=probe_grouped[c][:])
+
+            prof_grouped = {}
+
+            def prof_transposes(h):
+                for i in (2 * h, 2 * h + 1):
+                    grouped = work.tile([P, NG * P * PACK], BF16, name="prof_grouped%d" % (i % 2), align_bytes=64)
+                    prof_grouped[i] = grouped
+                    bank = psum_bank()
+                    words = prof_raw[h][:, i % 2, :].bitcast(F32)
+                    for g in range(NG):
+                        for u in range(2):
+                            x = 2 * g + u
+                            nc.tensor.transpose(
+                                bank[:, x * P:(x + 1) * P], words[:, 256 * g + u:256 * (g + 1):2], ident[:])
+                    nc.scalar.copy(
+                        out=grouped[:].bitcast(F32).rearrange("j (g r u) -> j g r u", g=NG, u=2),
+                        in_=bank[:].rearrange("j (g u r) -> j g r u", g=NG, u=2))
+
+            def prof_quantize(i):
+                nc.vector.quantize_mx(
+                    out=prof_codes[:, i].rearrange("p g r -> p (g r)").bitcast(FP8X4),
+                    scales=prof_scales[:, i].rearrange("p g r -> p (g r)"),
+                    in_=prof_grouped[i][:])
+
+            b_parts = {}
+
+            def first_stage(c, g):
+                parts = work.tile([P, PACK, NT], BF16, name="b_parts%d" % g)
+                b_parts[c, g] = parts
+                cols = slice(c * NT, (c + 1) * NT)
+                for t in range(PACK):
+                    s_cols = slice(g * KP + t * P, g * KP + (t + 1) * P)
+                    bank = psum_bank()
+                    nc.tensor.matmul_mx(
+                        out=bank[:],
+                        lhsT=seg_codes[:, s_cols].bitcast(FP8X4), lhsT_scale=seg_scales[:, s_cols],
+                        rhs=probe_codes[:, cols].bitcast(FP8X4), rhs_scale=probe_scales[:, cols],
+                        start=True, stop=True)
+                    k = g * PACK + t
+                    nc.scalar.activation(
+                        out=parts[:, t, :], in_=bank[:], func=ACT.Exp, bias=ln_act[:, k:k + 1])
+
+            b_grouped = {}
+
+            def b_interleave(c, g):
+                grouped = work.tile([P, NT * PACK], BF16, name="b_grouped%d" % g, align_bytes=64)
+                b_grouped[c, g] = grouped
+                interleave(grouped[:], b_parts[c, g][:])
+
+            def b_quantize(c, g):
+                cols = slice(c * NT, (c + 1) * NT)
+                nc.vector.quantize_mx(
+                    out=b_codes[:, g, cols].bitcast(FP8X4), scales=b_scales[:, g, cols], in_=b_grouped[c, g][:])
+
+            def second_stage(i, c0, width):
+                root = outp.tile([P, width], F32, name="root%d" % width)
+                for n in range(width // NT):
+                    cols = slice(c0 + n * NT, c0 + (n + 1) * NT)
+                    bank = psum_bank()
+                    for g in range(NG):
+                        nc.tensor.matmul_mx(
+                            out=bank[:],
+                            lhsT=prof_codes[:, i, g].bitcast(FP8X4), lhsT_scale=prof_scales[:, i, g],
+                            rhs=b_codes[:, g, cols].bitcast(FP8X4), rhs_scale=b_scales[:, g, cols],
+                            start=(g == 0), stop=(g == NG - 1))
+                    nc.scalar.activation(
+                        out=root[:, n * NT:(n + 1) * NT], in_=bank[:], func=ACT.Abs_reciprocal_sqrt)
+                result = outp.tile([P, width], F32, name="result%d" % width)
+                nc.vector.tensor_mul(out=result[:], in0=root[:], in1=root[:])
+                nc.sync.dma_start(out=out[i * P:(i + 1) * P, c0:c0 + width], in_=result[:])
+
+            seg_transposes(0)
+            probe_interleave(0)
+            seg_quantize(0)
+            probe_quantize(0)
+            seg_transposes(1)
+            probe_interleave(1)
+            seg_quantize(1)
+            first_stage(0, 0)
+            first_stage(0, 1)
+            probe_quantize(1)
+            prof_transposes(0)
+            b_interleave(0, 0)
+            probe_interleave(2)
+            b_quantize(0, 0)
+            b_interleave(0, 1)
+            probe_quantize(2)
+            first_stage(1, 0)
+            first_stage(1, 1)
+            prof_transposes(1)
+            prof_quantize(0)
+            b_quantize(0, 1)
+            prof_quantize(1)
+            b_interleave(1, 0)
+            probe_interleave(3)
+            b_quantize(1, 0)
+            b_interleave(1, 1)
+            probe_quantize(3)
+            first_stage(2, 0)
+            first_stage(2, 1)
+            prof_transposes(2)
+            prof_quantize(2)
+            b_quantize(1, 1)
+            prof_quantize(3)
+            b_interleave(2, 0)
+            prof_transposes(3)
+            prof_quantize(4)
+            b_quantize(2, 0)
+            b_interleave(2, 1)
+            prof_quantize(5)
+            first_stage(3, 0)
+            first_stage(3, 1)
+            b_quantize(2, 1)
+            prof_quantize(6)
+            prof_quantize(7)
+            b_interleave(3, 0)
+            b_interleave(3, 1)
+            b_quantize(3, 0)
+            b_quantize(3, 1)
+            for half in range(2):
+                for i in range(NI):
+                    if half == 1 and i == NI - 1:
+                        second_stage(i, Q // 2, NT)
+                        second_stage(i, Q // 2 + NT, NT)
+                    else:
+                        second_stage(i, half * (Q // 2), Q // 2)

@@ -16,10 +16,11 @@ ACT = mybir.ActivationFunctionType
 P = 128
 PACK = 4
 KP = P * PACK
-NT = 512
-NQ = Q // NT
+BANK = 512
 NG = S // KP
 NI = M // P
+CHUNKS = ((0, 256), (256, 256), (512, 512), (1024, 512), (1536, 512))
+HALVES = ((0, 1, 2), (3, 4))
 
 
 def tile_cosmo_segment_activities_s7_kernel(tc, seg, probe, act, prof, out):
@@ -27,7 +28,8 @@ def tile_cosmo_segment_activities_s7_kernel(tc, seg, probe, act, prof, out):
     with ExitStack() as ctx:
         keep = ctx.enter_context(tc.tile_pool(name="keep", bufs=1))
         work = ctx.enter_context(tc.tile_pool(name="work", bufs=2))
-        outp = ctx.enter_context(tc.tile_pool(name="outp", bufs=4))
+        outp = ctx.enter_context(tc.tile_pool(name="outp", bufs=3))
+        store = ctx.enter_context(tc.tile_pool(name="store", bufs=6))
         psum = ctx.enter_context(tc.psum_pool(name="psum", bufs=8))
 
         seg_view = seg.rearrange("(g p t) d -> g p t d", g=NG, t=PACK)
@@ -42,10 +44,10 @@ def tile_cosmo_segment_activities_s7_kernel(tc, seg, probe, act, prof, out):
         seg_scales = keep.tile([P, S], U8, name="seg_scales", align_bytes=64)
         probe_codes = keep.tile([P, Q], U32, name="probe_codes", align_bytes=64)
         probe_scales = keep.tile([P, Q], U8, name="probe_scales", align_bytes=64)
-        prof_codes = keep.tile([P, NI, NG, P], U32, name="prof_codes", align_bytes=64)
-        prof_scales = keep.tile([P, NI, NG, P], U8, name="prof_scales", align_bytes=64)
-        b_codes = keep.tile([P, NG, Q], U32, name="b_codes", align_bytes=64)
-        b_scales = keep.tile([P, NG, Q], U8, name="b_scales", align_bytes=64)
+        prof_codes = keep.tile([P, NI * NG * P], U32, name="prof_codes", align_bytes=64)
+        prof_scales = keep.tile([P, NI * NG * P], U8, name="prof_scales", align_bytes=64)
+        b_codes = keep.tile([P, NG * Q], U32, name="b_codes", align_bytes=64)
+        b_scales = keep.tile([P, NG * Q], U8, name="b_scales", align_bytes=64)
 
         one = keep.tile([P, 1], F32, name="one")
         junk = keep.tile([P, 1], F32, name="junk")
@@ -53,7 +55,7 @@ def tile_cosmo_segment_activities_s7_kernel(tc, seg, probe, act, prof, out):
         ln_act = keep.tile([P, NG * PACK], F32, name="ln_act")
 
         def psum_bank():
-            bank = psum.tile([P, NT], F32, name="bank")
+            bank = psum.tile([P, BANK], F32, name="bank")
             return bank
 
         with tc.manual_schedule():
@@ -61,27 +63,31 @@ def tile_cosmo_segment_activities_s7_kernel(tc, seg, probe, act, prof, out):
             nc.vector.memset(one[:], 1.0)
             nc.scalar.activation(out=junk[:], in_=one[:], func=ACT.Ln)
 
-            seg_raw = [keep.tile([P, PACK, D], BF16, name="seg_raw%d" % g) for g in range(NG)]
-            probe_raw = [keep.tile([P, PACK, NT], BF16, name="probe_raw%d" % c) for c in range(NQ)]
+            seg_raw = [[keep.tile([P, 2, D], BF16, name="seg_raw%d_%d" % (g, h)) for h in range(2)] for g in range(NG)]
+            probe_raw = [keep.tile([P, PACK, w], BF16, name="probe_raw%d" % q0) for q0, w in CHUNKS]
             prof_raw = [keep.tile([P, 2, S], BF16, name="prof_raw%d" % h) for h in range(NI // 2)]
 
-            def load_seg(g):
-                nc.sync.dma_start(out=seg_raw[g][:], in_=seg_view[g])
+            def load_seg(g, h):
+                nc.sync.dma_start(out=seg_raw[g][h][:], in_=seg_view[g][:, 2 * h:2 * h + 2, :])
 
             def load_probe(c):
-                nc.sync.dma_start(out=probe_raw[c][:], in_=probe_view[:, :, c * NT:(c + 1) * NT])
+                q0, w = CHUNKS[c]
+                nc.sync.dma_start(out=probe_raw[c][:], in_=probe_view[:, :, q0:q0 + w])
 
             def load_prof(h):
                 nc.sync.dma_start(out=prof_raw[h][:], in_=prof_view[:, 2 * h:2 * h + 2, :])
 
-            load_seg(0)
+            load_seg(0, 0)
             load_probe(0)
-            load_seg(1)
+            load_seg(0, 1)
+            load_seg(1, 0)
             load_probe(1)
-            load_prof(0)
+            load_seg(1, 1)
             load_probe(2)
-            load_prof(1)
+            load_prof(0)
             load_probe(3)
+            load_prof(1)
+            load_probe(4)
             load_prof(2)
             load_prof(3)
 
@@ -90,166 +96,210 @@ def tile_cosmo_segment_activities_s7_kernel(tc, seg, probe, act, prof, out):
 
             seg_grouped = {}
 
-            def seg_transposes(g):
-                grouped = work.tile([P, NT * PACK], BF16, name="seg_grouped", align_bytes=64)
-                seg_grouped[g] = grouped
-                words_out = grouped[:].bitcast(F32).rearrange("j (t p u) -> j t p u", t=PACK, u=2)
-                for half in range(2):
-                    bank = psum_bank()
-                    for k in range(2):
-                        words = seg_raw[g][:, 2 * half + k, :].bitcast(F32)
-                        for u in range(2):
-                            x = 2 * k + u
-                            nc.tensor.transpose(bank[:, x * P:(x + 1) * P], words[:, u::2], ident[:])
-                    nc.scalar.copy(
-                        out=words_out[:, 2 * half:2 * half + 2],
-                        in_=bank[:].rearrange("j (t u p) -> j t p u", t=2, u=2),
-                    )
+            def seg_transposes(g, h, copy):
+                grouped = work.tile([P, 2 * P * PACK], BF16, name="seg_grouped%d" % h, align_bytes=64)
+                seg_grouped[g, h] = grouped
+                bank = psum_bank()
+                for k in range(2):
+                    words = seg_raw[g][h][:, k, :].bitcast(F32)
+                    for u in range(2):
+                        x = 2 * k + u
+                        nc.tensor.transpose(bank[:, x * P:(x + 1) * P], words[:, u::2], ident[:])
+                copy(
+                    out=grouped[:].bitcast(F32).rearrange("j (t p u) -> j t p u", t=2, u=2),
+                    in_=bank[:].rearrange("j (t u p) -> j t p u", t=2, u=2),
+                )
 
-            def seg_quantize(g):
-                cols = slice(g * KP, (g + 1) * KP)
+            def seg_quantize(g, h):
+                c0 = g * KP + h * 2 * P
+                cols = slice(c0, c0 + 2 * P)
                 nc.vector.quantize_mx(
-                    out=seg_codes[:, cols].bitcast(FP8X4), scales=seg_scales[:, cols], in_=seg_grouped[g][:])
-
-            probe_grouped = {}
+                    out=seg_codes[:, cols].bitcast(FP8X4), scales=seg_scales[:, cols], in_=seg_grouped[g, h][:])
 
             def interleave(dst, src):
                 nc.vector.tensor_copy(
                     out=dst.rearrange("p (c i t) -> p c t i", i=4, t=PACK),
                     in_=src.rearrange("p t (c i) -> p c t i", i=4))
 
+            probe_grouped = {}
+
             def probe_interleave(c):
-                grouped = work.tile([P, NT * PACK], BF16, name="probe_grouped", align_bytes=64)
+                q0, w = CHUNKS[c]
+                grouped = work.tile([P, w * PACK], BF16, name="probe_grouped%d" % w, align_bytes=64)
                 probe_grouped[c] = grouped
                 interleave(grouped[:], probe_raw[c][:])
 
             def probe_quantize(c):
-                cols = slice(c * NT, (c + 1) * NT)
+                q0, w = CHUNKS[c]
+                cols = slice(q0, q0 + w)
                 nc.vector.quantize_mx(
                     out=probe_codes[:, cols].bitcast(FP8X4), scales=probe_scales[:, cols], in_=probe_grouped[c][:])
 
             prof_grouped = {}
 
-            def prof_transposes(h):
-                for i in (2 * h, 2 * h + 1):
-                    grouped = work.tile([P, NG * P * PACK], BF16, name="prof_grouped%d" % (i % 2), align_bytes=64)
-                    prof_grouped[i] = grouped
+            def prof_transposes(h, copies=(nc.scalar.copy, nc.scalar.copy)):
+                grouped = work.tile([P, 2, NG * P * PACK], BF16, name="prof_grouped", align_bytes=64)
+                prof_grouped[h] = grouped
+                for i in range(2):
                     bank = psum_bank()
-                    words = prof_raw[h][:, i % 2, :].bitcast(F32)
+                    words = prof_raw[h][:, i, :].bitcast(F32)
                     for g in range(NG):
                         for u in range(2):
                             x = 2 * g + u
                             nc.tensor.transpose(
                                 bank[:, x * P:(x + 1) * P], words[:, 256 * g + u:256 * (g + 1):2], ident[:])
-                    nc.scalar.copy(
-                        out=grouped[:].bitcast(F32).rearrange("j (g r u) -> j g r u", g=NG, u=2),
+                    copies[i](
+                        out=grouped[:, i, :].bitcast(F32).rearrange("j (g r u) -> j g r u", g=NG, u=2),
                         in_=bank[:].rearrange("j (g u r) -> j g r u", g=NG, u=2))
 
-            def prof_quantize(i):
+            def prof_quantize(h):
+                cols = slice(2 * h * NG * P, 2 * (h + 1) * NG * P)
                 nc.vector.quantize_mx(
-                    out=prof_codes[:, i].rearrange("p g r -> p (g r)").bitcast(FP8X4),
-                    scales=prof_scales[:, i].rearrange("p g r -> p (g r)"),
-                    in_=prof_grouped[i][:])
+                    out=prof_codes[:, cols].bitcast(FP8X4), scales=prof_scales[:, cols],
+                    in_=prof_grouped[h][:].rearrange("p i n -> p (i n)"))
 
             b_parts = {}
 
-            def first_stage(c, g):
-                parts = work.tile([P, PACK, NT], BF16, name="b_parts%d" % g)
-                b_parts[c, g] = parts
-                cols = slice(c * NT, (c + 1) * NT)
-                for t in range(PACK):
+            def first_stage(c, g, ts=range(PACK)):
+                q0, w = CHUNKS[c]
+                if (c, g) not in b_parts:
+                    parts = work.tile([P, PACK, w], BF16, name="b_parts%d_%d" % (g, w))
+                    b_parts[c, g] = parts
+                parts = b_parts[c, g]
+                cols = slice(q0, q0 + w)
+                for t in ts:
                     s_cols = slice(g * KP + t * P, g * KP + (t + 1) * P)
                     bank = psum_bank()
                     nc.tensor.matmul_mx(
-                        out=bank[:],
+                        out=bank[:, 0:w],
                         lhsT=seg_codes[:, s_cols].bitcast(FP8X4), lhsT_scale=seg_scales[:, s_cols],
                         rhs=probe_codes[:, cols].bitcast(FP8X4), rhs_scale=probe_scales[:, cols],
                         start=True, stop=True)
                     k = g * PACK + t
                     nc.scalar.activation(
-                        out=parts[:, t, :], in_=bank[:], func=ACT.Exp, bias=ln_act[:, k:k + 1])
+                        out=parts[:, t, :], in_=bank[:, 0:w], func=ACT.Exp, bias=ln_act[:, k:k + 1])
 
             b_grouped = {}
 
             def b_interleave(c, g):
-                grouped = work.tile([P, NT * PACK], BF16, name="b_grouped%d" % g, align_bytes=64)
-                b_grouped[c, g] = grouped
-                interleave(grouped[:], b_parts[c, g][:])
+                q0, w = CHUNKS[c]
+                if g == 0:
+                    grouped = work.tile([P, NG, w * PACK], BF16, name="b_grouped%d" % w, align_bytes=64)
+                    b_grouped[c] = grouped
+                interleave(b_grouped[c][:, g, :], b_parts[c, g][:])
 
-            def b_quantize(c, g):
-                cols = slice(c * NT, (c + 1) * NT)
+            def b_quantize(c):
+                q0, w = CHUNKS[c]
+                cols = slice(NG * q0, NG * (q0 + w))
                 nc.vector.quantize_mx(
-                    out=b_codes[:, g, cols].bitcast(FP8X4), scales=b_scales[:, g, cols], in_=b_grouped[c, g][:])
+                    out=b_codes[:, cols].bitcast(FP8X4), scales=b_scales[:, cols],
+                    in_=b_grouped[c][:].rearrange("p g n -> p (g n)"))
 
-            def second_stage(i, c0, width):
-                root = outp.tile([P, width], F32, name="root%d" % width)
-                for n in range(width // NT):
-                    cols = slice(c0 + n * NT, c0 + (n + 1) * NT)
+            def z_columns(i, c, bank, offset):
+                q0, w = CHUNKS[c]
+                for g in range(NG):
+                    s_cols = slice((i * NG + g) * P, (i * NG + g + 1) * P)
+                    cols = slice(NG * q0 + g * w, NG * q0 + (g + 1) * w)
+                    nc.tensor.matmul_mx(
+                        out=bank[:, offset:offset + w],
+                        lhsT=prof_codes[:, s_cols].bitcast(FP8X4), lhsT_scale=prof_scales[:, s_cols],
+                        rhs=b_codes[:, cols].bitcast(FP8X4), rhs_scale=b_scales[:, cols],
+                        start=(g == 0), stop=(g == NG - 1))
+
+            roots = {}
+
+            def second_stage(i, banks):
+                if i not in roots:
+                    root = outp.tile([P, Q], F32, name="root")
+                    roots[i] = root
+                for n in banks:
                     bank = psum_bank()
-                    for g in range(NG):
-                        nc.tensor.matmul_mx(
-                            out=bank[:],
-                            lhsT=prof_codes[:, i, g].bitcast(FP8X4), lhsT_scale=prof_scales[:, i, g],
-                            rhs=b_codes[:, g, cols].bitcast(FP8X4), rhs_scale=b_scales[:, g, cols],
-                            start=(g == 0), stop=(g == NG - 1))
+                    for c, (q0, w) in enumerate(CHUNKS):
+                        if q0 // BANK == n:
+                            z_columns(i, c, bank, q0 % BANK)
                     nc.scalar.activation(
-                        out=root[:, n * NT:(n + 1) * NT], in_=bank[:], func=ACT.Abs_reciprocal_sqrt)
-                result = outp.tile([P, width], F32, name="result%d" % width)
-                nc.vector.tensor_mul(out=result[:], in0=root[:], in1=root[:])
-                nc.sync.dma_start(out=out[i * P:(i + 1) * P, c0:c0 + width], in_=result[:])
+                        out=roots[i][:, n * BANK:(n + 1) * BANK], in_=bank[:], func=ACT.Abs_reciprocal_sqrt)
 
-            seg_transposes(0)
+            def finish(i, q0, w, by_scalar=False):
+                result = store.tile([P, w], F32, name="result%d" % w)
+                root = roots[i][:, q0:q0 + w]
+                if by_scalar:
+                    nc.scalar.activation(out=result[:], in_=root, func=ACT.Square)
+                else:
+                    nc.vector.tensor_mul(out=result[:], in0=root, in1=root)
+                nc.sync.dma_start(out=out[i * P:(i + 1) * P, q0:q0 + w], in_=result[:])
+
+            seg_transposes(0, 0, nc.scalar.copy)
             probe_interleave(0)
-            seg_quantize(0)
             probe_quantize(0)
-            seg_transposes(1)
+            seg_quantize(0, 0)
+            seg_transposes(0, 1, nc.scalar.copy)
+            seg_quantize(0, 1)
+            first_stage(0, 0, (0, 1))
+            seg_transposes(1, 0, nc.scalar.copy)
+            first_stage(0, 0, (2, 3))
             probe_interleave(1)
-            seg_quantize(1)
-            first_stage(0, 0)
-            first_stage(0, 1)
+            seg_quantize(1, 0)
             probe_quantize(1)
-            prof_transposes(0)
+            seg_transposes(1, 1, nc.scalar.copy)
             b_interleave(0, 0)
-            probe_interleave(2)
-            b_quantize(0, 0)
-            b_interleave(0, 1)
-            probe_quantize(2)
+            seg_quantize(1, 1)
             first_stage(1, 0)
+            first_stage(0, 1)
             first_stage(1, 1)
-            prof_transposes(1)
-            prof_quantize(0)
-            b_quantize(0, 1)
-            prof_quantize(1)
+            probe_interleave(2)
             b_interleave(1, 0)
-            probe_interleave(3)
-            b_quantize(1, 0)
-            b_interleave(1, 1)
-            probe_quantize(3)
+            probe_quantize(2)
+            b_interleave(0, 1)
+            prof_transposes(0)
             first_stage(2, 0)
             first_stage(2, 1)
-            prof_transposes(2)
-            prof_quantize(2)
-            b_quantize(1, 1)
-            prof_quantize(3)
-            b_interleave(2, 0)
-            prof_transposes(3)
-            prof_quantize(4)
-            b_quantize(2, 0)
-            b_interleave(2, 1)
-            prof_quantize(5)
+            probe_interleave(3)
+            b_quantize(0)
+            b_interleave(1, 1)
+            probe_quantize(3)
+            prof_quantize(0)
+            b_quantize(1)
             first_stage(3, 0)
             first_stage(3, 1)
-            b_quantize(2, 1)
-            prof_quantize(6)
-            prof_quantize(7)
+            probe_interleave(4)
+            b_interleave(2, 0)
+            probe_quantize(4)
+            b_interleave(2, 1)
+            first_stage(4, 0)
+            first_stage(4, 1)
             b_interleave(3, 0)
+            b_quantize(2)
             b_interleave(3, 1)
-            b_quantize(3, 0)
-            b_quantize(3, 1)
-            for half in range(2):
-                for i in range(NI):
-                    if half == 1 and i == NI - 1:
-                        second_stage(i, Q // 2, NT)
-                        second_stage(i, Q // 2 + NT, NT)
-                    else:
-                        second_stage(i, half * (Q // 2), Q // 2)
+            b_interleave(4, 0)
+            b_quantize(3)
+            b_interleave(4, 1)
+            second_stage(0, (0, 1))
+            second_stage(1, (0, 1))
+            b_quantize(4)
+            finish(0, 0, 1024)
+            prof_transposes(1)
+            finish(1, 0, 1024)
+            second_stage(0, (2, 3))
+            second_stage(1, (2, 3))
+            prof_quantize(1)
+            prof_transposes(2, (nc.scalar.copy, nc.vector.tensor_copy))
+            finish(0, 1024, 1024)
+            finish(1, 1024, 1024)
+            second_stage(2, range(4))
+            prof_quantize(2)
+            finish(2, 0, 1024)
+            finish(2, 1024, 1024)
+            prof_transposes(3)
+            second_stage(3, range(4))
+            finish(3, 0, 1024)
+            prof_quantize(3)
+            finish(3, 1024, 1024)
+            for i in (4, 5, 6):
+                second_stage(i, range(4))
+                finish(i, 0, 1024)
+                finish(i, 1024, 1024)
+            second_stage(7, range(4))
+            finish(7, 0, 1024)
+            finish(7, 1024, 512)
+            finish(7, 1536, 512, True)

@@ -20,7 +20,7 @@ BANK = 512
 NG = S // KP
 NI = M // P
 CHUNKS = ((0, 256), (256, 256), (512, 512), (1024, 512), (1536, 512))
-HALVES = ((0, 1, 2), (3, 4))
+LOADS = ((0, 256), (256, 256), (512, 512), (1024, 1024))
 
 
 def tile_cosmo_segment_activities_s7_kernel(tc, seg, probe, act, prof, out):
@@ -28,7 +28,7 @@ def tile_cosmo_segment_activities_s7_kernel(tc, seg, probe, act, prof, out):
     with ExitStack() as ctx:
         keep = ctx.enter_context(tc.tile_pool(name="keep", bufs=1))
         work = ctx.enter_context(tc.tile_pool(name="work", bufs=2))
-        outp = ctx.enter_context(tc.tile_pool(name="outp", bufs=3))
+        outp = ctx.enter_context(tc.tile_pool(name="outp", bufs=4))
         store = ctx.enter_context(tc.tile_pool(name="store", bufs=6))
         psum = ctx.enter_context(tc.psum_pool(name="psum", bufs=8))
 
@@ -64,14 +64,14 @@ def tile_cosmo_segment_activities_s7_kernel(tc, seg, probe, act, prof, out):
             nc.scalar.activation(out=junk[:], in_=one[:], func=ACT.Ln)
 
             seg_raw = [[keep.tile([P, 2, D], BF16, name="seg_raw%d_%d" % (g, h)) for h in range(2)] for g in range(NG)]
-            probe_raw = [keep.tile([P, PACK, w], BF16, name="probe_raw%d" % q0) for q0, w in CHUNKS]
+            probe_raw = [keep.tile([P, PACK, w], BF16, name="probe_raw%d" % q0) for q0, w in LOADS]
             prof_raw = [keep.tile([P, 2, S], BF16, name="prof_raw%d" % h) for h in range(NI // 2)]
 
             def load_seg(g, h):
                 nc.sync.dma_start(out=seg_raw[g][h][:], in_=seg_view[g][:, 2 * h:2 * h + 2, :])
 
             def load_probe(c):
-                q0, w = CHUNKS[c]
+                q0, w = LOADS[c]
                 nc.sync.dma_start(out=probe_raw[c][:], in_=probe_view[:, :, q0:q0 + w])
 
             def load_prof(h):
@@ -87,30 +87,32 @@ def tile_cosmo_segment_activities_s7_kernel(tc, seg, probe, act, prof, out):
             load_prof(0)
             load_probe(3)
             load_prof(1)
-            load_probe(4)
             load_prof(2)
             load_prof(3)
 
             nc.scalar.activation(out=ln_act[:], in_=act_sb[:].rearrange("p g t -> p (g t)"), func=ACT.Ln)
             nc.scalar.activation(out=junk[:], in_=one[:], func=ACT.Exp)
 
+            seg_bank = {}
             seg_grouped = {}
 
-            def seg_transposes(g, h, copy):
-                grouped = work.tile([P, 2 * P * PACK], BF16, name="seg_grouped%d" % h, align_bytes=64)
-                seg_grouped[g, h] = grouped
+            def seg_t(g, h):
                 bank = psum_bank()
+                seg_bank[g, h] = bank
                 for k in range(2):
                     words = seg_raw[g][h][:, k, :].bitcast(F32)
                     for u in range(2):
                         x = 2 * k + u
                         nc.tensor.transpose(bank[:, x * P:(x + 1) * P], words[:, u::2], ident[:])
+
+            def seg_c(g, h, copy):
+                grouped = work.tile([P, 2 * P * PACK], BF16, name="seg_grouped%d" % h, align_bytes=64)
+                seg_grouped[g, h] = grouped
                 copy(
                     out=grouped[:].bitcast(F32).rearrange("j (t p u) -> j t p u", t=2, u=2),
-                    in_=bank[:].rearrange("j (t u p) -> j t p u", t=2, u=2),
-                )
+                    in_=seg_bank[g, h][:].rearrange("j (t u p) -> j t p u", t=2, u=2))
 
-            def seg_quantize(g, h):
+            def seg_q(g, h):
                 c0 = g * KP + h * 2 * P
                 cols = slice(c0, c0 + 2 * P)
                 nc.vector.quantize_mx(
@@ -123,36 +125,42 @@ def tile_cosmo_segment_activities_s7_kernel(tc, seg, probe, act, prof, out):
 
             probe_grouped = {}
 
-            def probe_interleave(c):
+            def p_i(c):
                 q0, w = CHUNKS[c]
                 grouped = work.tile([P, w * PACK], BF16, name="probe_grouped%d" % w, align_bytes=64)
                 probe_grouped[c] = grouped
-                interleave(grouped[:], probe_raw[c][:])
+                k = min(c, len(LOADS) - 1)
+                first = q0 - LOADS[k][0]
+                interleave(grouped[:], probe_raw[k][:, :, first:first + w])
 
-            def probe_quantize(c):
+            def p_q(c):
                 q0, w = CHUNKS[c]
                 cols = slice(q0, q0 + w)
                 nc.vector.quantize_mx(
                     out=probe_codes[:, cols].bitcast(FP8X4), scales=probe_scales[:, cols], in_=probe_grouped[c][:])
 
+            prof_bank = {}
             prof_grouped = {}
 
-            def prof_transposes(h, copies=(nc.scalar.copy, nc.scalar.copy)):
-                grouped = work.tile([P, 2, NG * P * PACK], BF16, name="prof_grouped", align_bytes=64)
-                prof_grouped[h] = grouped
-                for i in range(2):
-                    bank = psum_bank()
-                    words = prof_raw[h][:, i, :].bitcast(F32)
-                    for g in range(NG):
-                        for u in range(2):
-                            x = 2 * g + u
-                            nc.tensor.transpose(
-                                bank[:, x * P:(x + 1) * P], words[:, 256 * g + u:256 * (g + 1):2], ident[:])
-                    copies[i](
-                        out=grouped[:, i, :].bitcast(F32).rearrange("j (g r u) -> j g r u", g=NG, u=2),
-                        in_=bank[:].rearrange("j (g u r) -> j g r u", g=NG, u=2))
+            def prof_t(i):
+                bank = psum_bank()
+                prof_bank[i] = bank
+                words = prof_raw[i // 2][:, i % 2, :].bitcast(F32)
+                for g in range(NG):
+                    for u in range(2):
+                        x = 2 * g + u
+                        nc.tensor.transpose(
+                            bank[:, x * P:(x + 1) * P], words[:, 256 * g + u:256 * (g + 1):2], ident[:])
 
-            def prof_quantize(h):
+            def prof_c(i, copy):
+                if i % 2 == 0:
+                    grouped = work.tile([P, 2, NG * P * PACK], BF16, name="prof_grouped", align_bytes=64)
+                    prof_grouped[i // 2] = grouped
+                copy(
+                    out=prof_grouped[i // 2][:, i % 2, :].bitcast(F32).rearrange("j (g r u) -> j g r u", g=NG, u=2),
+                    in_=prof_bank[i][:].rearrange("j (g u r) -> j g r u", g=NG, u=2))
+
+            def prof_q(h):
                 cols = slice(2 * h * NG * P, 2 * (h + 1) * NG * P)
                 nc.vector.quantize_mx(
                     out=prof_codes[:, cols].bitcast(FP8X4), scales=prof_scales[:, cols],
@@ -160,146 +168,182 @@ def tile_cosmo_segment_activities_s7_kernel(tc, seg, probe, act, prof, out):
 
             b_parts = {}
 
-            def first_stage(c, g, ts=range(PACK)):
+            def e(c, g, t):
                 q0, w = CHUNKS[c]
                 if (c, g) not in b_parts:
                     parts = work.tile([P, PACK, w], BF16, name="b_parts%d_%d" % (g, w))
                     b_parts[c, g] = parts
-                parts = b_parts[c, g]
                 cols = slice(q0, q0 + w)
-                for t in ts:
-                    s_cols = slice(g * KP + t * P, g * KP + (t + 1) * P)
-                    bank = psum_bank()
-                    nc.tensor.matmul_mx(
-                        out=bank[:, 0:w],
-                        lhsT=seg_codes[:, s_cols].bitcast(FP8X4), lhsT_scale=seg_scales[:, s_cols],
-                        rhs=probe_codes[:, cols].bitcast(FP8X4), rhs_scale=probe_scales[:, cols],
-                        start=True, stop=True)
-                    k = g * PACK + t
-                    nc.scalar.activation(
-                        out=parts[:, t, :], in_=bank[:, 0:w], func=ACT.Exp, bias=ln_act[:, k:k + 1])
+                s_cols = slice(g * KP + t * P, g * KP + (t + 1) * P)
+                bank = psum_bank()
+                nc.tensor.matmul_mx(
+                    out=bank[:, 0:w],
+                    lhsT=seg_codes[:, s_cols].bitcast(FP8X4), lhsT_scale=seg_scales[:, s_cols],
+                    rhs=probe_codes[:, cols].bitcast(FP8X4), rhs_scale=probe_scales[:, cols],
+                    start=True, stop=True)
+                k = g * PACK + t
+                nc.scalar.activation(
+                    out=b_parts[c, g][:, t, :], in_=bank[:, 0:w], func=ACT.Exp, bias=ln_act[:, k:k + 1])
 
             b_grouped = {}
 
-            def b_interleave(c, g):
+            def b_i(c, g):
                 q0, w = CHUNKS[c]
                 if g == 0:
                     grouped = work.tile([P, NG, w * PACK], BF16, name="b_grouped%d" % w, align_bytes=64)
                     b_grouped[c] = grouped
                 interleave(b_grouped[c][:, g, :], b_parts[c, g][:])
 
-            def b_quantize(c):
+            def b_q(c):
                 q0, w = CHUNKS[c]
                 cols = slice(NG * q0, NG * (q0 + w))
                 nc.vector.quantize_mx(
                     out=b_codes[:, cols].bitcast(FP8X4), scales=b_scales[:, cols],
                     in_=b_grouped[c][:].rearrange("p g n -> p (g n)"))
 
-            def z_columns(i, c, bank, offset):
-                q0, w = CHUNKS[c]
-                for g in range(NG):
-                    s_cols = slice((i * NG + g) * P, (i * NG + g + 1) * P)
-                    cols = slice(NG * q0 + g * w, NG * q0 + (g + 1) * w)
-                    nc.tensor.matmul_mx(
-                        out=bank[:, offset:offset + w],
-                        lhsT=prof_codes[:, s_cols].bitcast(FP8X4), lhsT_scale=prof_scales[:, s_cols],
-                        rhs=b_codes[:, cols].bitcast(FP8X4), rhs_scale=b_scales[:, cols],
-                        start=(g == 0), stop=(g == NG - 1))
-
             roots = {}
 
-            def second_stage(i, banks):
-                if i not in roots:
-                    root = outp.tile([P, Q], F32, name="root")
-                    roots[i] = root
-                for n in banks:
-                    bank = psum_bank()
-                    for c, (q0, w) in enumerate(CHUNKS):
-                        if q0 // BANK == n:
-                            z_columns(i, c, bank, q0 % BANK)
+            def z(i, n, pieces=1):
+                half = n // 2
+                if (i, half) not in roots:
+                    root = outp.tile([P, 2 * BANK], F32, name="root")
+                    roots[i, half] = root
+                bank = psum_bank()
+                for q0, w in CHUNKS:
+                    if q0 // BANK == n:
+                        for g in range(NG):
+                            s_cols = slice((i * NG + g) * P, (i * NG + g + 1) * P)
+                            cols = slice(NG * q0 + g * w, NG * q0 + (g + 1) * w)
+                            nc.tensor.matmul_mx(
+                                out=bank[:, q0 % BANK:q0 % BANK + w],
+                                lhsT=prof_codes[:, s_cols].bitcast(FP8X4), lhsT_scale=prof_scales[:, s_cols],
+                                rhs=b_codes[:, cols].bitcast(FP8X4), rhs_scale=b_scales[:, cols],
+                                start=(g == 0), stop=(g == NG - 1))
+                step = BANK // pieces
+                for x in range(0, BANK, step):
+                    r0 = (n % 2) * BANK + x
                     nc.scalar.activation(
-                        out=roots[i][:, n * BANK:(n + 1) * BANK], in_=bank[:], func=ACT.Abs_reciprocal_sqrt)
+                        out=roots[i, half][:, r0:r0 + step], in_=bank[:, x:x + step], func=ACT.Abs_reciprocal_sqrt)
 
-            def finish(i, q0, w, by_scalar=False):
+            def sq(i, half, r0, w, scalar=0):
                 result = store.tile([P, w], F32, name="result%d" % w)
-                root = roots[i][:, q0:q0 + w]
-                if by_scalar:
+                root = roots[i, half][:, r0:r0 + w]
+                if scalar:
                     nc.scalar.activation(out=result[:], in_=root, func=ACT.Square)
                 else:
                     nc.vector.tensor_mul(out=result[:], in0=root, in1=root)
+                q0 = half * 2 * BANK + r0
                 nc.sync.dma_start(out=out[i * P:(i + 1) * P, q0:q0 + w], in_=result[:])
 
-            seg_transposes(0, 0, nc.scalar.copy)
-            probe_interleave(0)
-            probe_quantize(0)
-            seg_quantize(0, 0)
-            seg_transposes(0, 1, nc.scalar.copy)
-            seg_quantize(0, 1)
-            first_stage(0, 0, (0, 1))
-            seg_transposes(1, 0, nc.scalar.copy)
-            first_stage(0, 0, (2, 3))
-            probe_interleave(1)
-            seg_quantize(1, 0)
-            probe_quantize(1)
-            seg_transposes(1, 1, nc.scalar.copy)
-            b_interleave(0, 0)
-            seg_quantize(1, 1)
-            first_stage(1, 0)
-            first_stage(0, 1)
-            first_stage(1, 1)
-            probe_interleave(2)
-            b_interleave(1, 0)
-            probe_quantize(2)
-            b_interleave(0, 1)
-            prof_transposes(0)
-            first_stage(2, 0)
-            first_stage(2, 1)
-            probe_interleave(3)
-            b_quantize(0)
-            b_interleave(1, 1)
-            probe_quantize(3)
-            prof_quantize(0)
-            b_quantize(1)
-            first_stage(3, 0)
-            first_stage(3, 1)
-            probe_interleave(4)
-            b_interleave(2, 0)
-            probe_quantize(4)
-            b_interleave(2, 1)
-            first_stage(4, 0)
-            first_stage(4, 1)
-            b_interleave(3, 0)
-            b_quantize(2)
-            b_interleave(3, 1)
-            b_interleave(4, 0)
-            b_quantize(3)
-            b_interleave(4, 1)
-            second_stage(0, (0, 1))
-            second_stage(1, (0, 1))
-            b_quantize(4)
-            finish(0, 0, 1024)
-            prof_transposes(1)
-            finish(1, 0, 1024)
-            second_stage(0, (2, 3))
-            second_stage(1, (2, 3))
-            prof_quantize(1)
-            prof_transposes(2, (nc.scalar.copy, nc.vector.tensor_copy))
-            finish(0, 1024, 1024)
-            finish(1, 1024, 1024)
-            second_stage(2, range(4))
-            prof_quantize(2)
-            finish(2, 0, 1024)
-            finish(2, 1024, 1024)
-            prof_transposes(3)
-            second_stage(3, range(4))
-            finish(3, 0, 1024)
-            prof_quantize(3)
-            finish(3, 1024, 1024)
-            for i in (4, 5, 6):
-                second_stage(i, range(4))
-                finish(i, 0, 1024)
-                finish(i, 1024, 1024)
-            second_stage(7, range(4))
-            finish(7, 0, 1024)
-            finish(7, 1024, 512)
-            finish(7, 1536, 512, True)
+            def E(c, g, ts=range(PACK)):
+                for t in ts:
+                    e(c, g, t)
+
+            def Z(i, half, pieces=1):
+                z(i, 2 * half)
+                z(i, 2 * half + 1, pieces)
+
+            V = nc.vector.tensor_copy
+            A = nc.scalar.copy
+            p_i(0)
+            seg_t(0, 0)
+            seg_t(0, 1)
+            seg_t(1, 0)
+            seg_c(0, 0, V)
+            p_q(0)
+            seg_q(0, 0)
+            seg_c(0, 1, A)
+            seg_c(1, 0, A)
+            seg_q(0, 1)
+            p_i(1)
+            E(0, 0)
+            seg_q(1, 0)
+            seg_t(1, 1)
+            seg_c(1, 1, A)
+            p_q(1)
+            p_i(2)
+            seg_q(1, 1)
+            b_i(0, 0)
+            E(1, 0)
+            b_i(1, 0)
+            p_q(2)
+            E(1, 1)
+            E(0, 1)
+            b_i(1, 1)
+            b_i(0, 1)
+            E(2, 0)
+            prof_t(0)
+            E(2, 1)
+            p_i(3)
+            p_i(4)
+            p_q(3)
+            prof_c(0, V)
+            prof_t(1)
+            p_q(4)
+            b_i(2, 0)
+            prof_c(1, A)
+            b_i(2, 1)
+            E(3, 0)
+            E(4, 0)
+            prof_t(2)
+            prof_t(3)
+            E(3, 1)
+            prof_c(2, V)
+            prof_c(3, V)
+            prof_q(0)
+            E(4, 1)
+            prof_t(4)
+            prof_t(5)
+            b_q(0)
+            b_q(2)
+            prof_q(1)
+            b_q(1)
+            b_i(4, 0)
+            Z(0, 0)
+            prof_c(4, V)
+            Z(1, 0)
+            prof_t(6)
+            prof_t(7)
+            b_i(3, 0)
+            prof_c(6, V)
+            b_i(3, 1)
+            prof_c(5, V)
+            sq(0, 0, 0, 1024)
+            Z(2, 0)
+            prof_q(2)
+            sq(1, 0, 0, 1024, 1)
+            prof_c(7, A)
+            sq(2, 0, 0, 1024)
+            b_i(4, 1)
+            prof_q(3)
+            b_q(4)
+            Z(3, 0)
+            Z(4, 0)
+            sq(3, 0, 0, 1024, 1)
+            Z(5, 0)
+            Z(6, 0)
+            b_q(3)
+            sq(4, 0, 0, 1024)
+            Z(7, 0)
+            sq(5, 0, 0, 1024)
+            Z(0, 1)
+            sq(6, 0, 0, 1024)
+            Z(1, 1)
+            sq(7, 0, 0, 1024)
+            Z(2, 1)
+            sq(0, 1, 0, 1024)
+            Z(3, 1)
+            sq(1, 1, 0, 1024)
+            Z(4, 1)
+            sq(2, 1, 0, 1024)
+            Z(5, 1)
+            sq(3, 1, 0, 1024)
+            Z(6, 1)
+            sq(4, 1, 0, 1024)
+            z(7, 2)
+            z(7, 3, 2)
+            sq(5, 1, 0, 1024)
+            sq(7, 1, 0, 512)
+            sq(7, 1, 512, 256, 1)
+            sq(7, 1, 768, 256, 1)
+            sq(6, 1, 0, 1024, 1)

@@ -1,3 +1,4 @@
+import math
 from contextlib import ExitStack
 
 import concourse.mybir as mybir
@@ -8,19 +9,29 @@ FLOPS = 2 * S * D * Q + 2 * M * S * Q
 
 F32 = mybir.dt.float32
 BF16 = mybir.dt.bfloat16
+I32 = mybir.dt.int32
 U32 = mybir.dt.uint32
 U8 = mybir.dt.uint8
 FP8X4 = mybir.dt.float8_e4m3fn_x4
 ACT = mybir.ActivationFunctionType
+ALU = mybir.AluOpType
 
 P = 128
 PACK = 4
-KP = P * PACK
+PASS = P * PACK
 BANK = 512
-NG = S // KP
+NG = S // PASS
 NI = M // P
+HALF = Q // 2
+
 CHUNKS = ((0, 256), (256, 256), (512, 512), (1024, 512), (1536, 512))
-LOADS = ((0, 256), (256, 256), (512, 512), (1024, 1024))
+PROBE_LOADS = ((0, 256), (256, 256), (512, 512), (1024, 1024))
+
+MANTISSA_BITS = 0x007FFFFF
+BITS_OF_ONE = 0x3F800000
+MANTISSA_WIDTH = 23
+EXPONENT_MASK = 0xFF
+EXPONENT_BIAS = 127.0
 
 
 def tile_cosmo_segment_activities_s7_kernel(tc, seg, probe, act, prof, out):
@@ -28,17 +39,17 @@ def tile_cosmo_segment_activities_s7_kernel(tc, seg, probe, act, prof, out):
     with ExitStack() as ctx:
         keep = ctx.enter_context(tc.tile_pool(name="keep", bufs=1))
         work = ctx.enter_context(tc.tile_pool(name="work", bufs=2))
-        outp = ctx.enter_context(tc.tile_pool(name="outp", bufs=4))
-        store = ctx.enter_context(tc.tile_pool(name="store", bufs=6))
+        root_pool = ctx.enter_context(tc.tile_pool(name="root_pool", bufs=4))
+        result_pool = ctx.enter_context(tc.tile_pool(name="result_pool", bufs=6))
         psum = ctx.enter_context(tc.psum_pool(name="psum", bufs=8))
 
         seg_view = seg.rearrange("(g p t) d -> g p t d", g=NG, t=PACK)
-        probe_view = probe.rearrange("(p j) q -> p j q", j=PACK)
+        probe_view = probe.rearrange("(p t) q -> p t q", t=PACK)
         prof_view = prof.rearrange("(i r) s -> r i s", r=P)
         act_view = act.rearrange("(g p t) -> p g t", g=NG, t=PACK)
 
-        ident = keep.tile([P, P], F32, name="ident")
-        make_identity(nc, ident[:])
+        identity = keep.tile([P, P], F32, name="identity")
+        make_identity(nc, identity[:])
 
         seg_codes = keep.tile([P, S], U32, name="seg_codes", align_bytes=64)
         seg_scales = keep.tile([P, S], U8, name="seg_scales", align_bytes=64)
@@ -49,33 +60,208 @@ def tile_cosmo_segment_activities_s7_kernel(tc, seg, probe, act, prof, out):
         b_codes = keep.tile([P, NG * Q], U32, name="b_codes", align_bytes=64)
         b_scales = keep.tile([P, NG * Q], U8, name="b_scales", align_bytes=64)
 
-        one = keep.tile([P, 1], F32, name="one")
-        junk = keep.tile([P, 1], F32, name="junk")
-        act_sb = keep.tile([P, NG, PACK], BF16, name="act_sb")
-        ln_act = keep.tile([P, NG * PACK], F32, name="ln_act")
+        seg_raw = [[keep.tile([P, 2, D], BF16, name="seg_raw%d_%d" % (g, h)) for h in range(2)] for g in range(NG)]
+        probe_raw = [keep.tile([P, PACK, w], BF16, name="probe_raw%d" % q0) for q0, w in PROBE_LOADS]
+        prof_raw = [keep.tile([P, 2, S], BF16, name="prof_raw%d" % h) for h in range(NI // 2)]
 
-        def psum_bank():
+        act_raw = keep.tile([P, NG, PACK], BF16, name="act_raw")
+        act_f32 = keep.tile([P, NG * PACK], F32, name="act_f32")
+        mantissa = keep.tile([P, NG * PACK], I32, name="mantissa")
+        exponent = keep.tile([P, NG * PACK], I32, name="exponent")
+        ln_mantissa = keep.tile([P, NG * PACK], F32, name="ln_mantissa")
+        ln_power = keep.tile([P, NG * PACK], F32, name="ln_power")
+        ln_act = keep.tile([P, NG * PACK], F32, name="ln_act")
+        one = keep.tile([P, 1], F32, name="one")
+        unused = keep.tile([P, 1], F32, name="unused")
+
+        def new_bank():
             bank = psum.tile([P, BANK], F32, name="bank")
             return bank
 
+        def load_seg(g, h):
+            nc.sync.dma_start(out=seg_raw[g][h][:], in_=seg_view[g][:, 2 * h:2 * h + 2, :])
+
+        def load_probe(n):
+            q0, w = PROBE_LOADS[n]
+            nc.sync.dma_start(out=probe_raw[n][:], in_=probe_view[:, :, q0:q0 + w])
+
+        def load_prof(h):
+            nc.sync.dma_start(out=prof_raw[h][:], in_=prof_view[:, 2 * h:2 * h + 2, :])
+
+        def make_ln_act():
+            nc.vector.tensor_copy(out=act_f32[:], in_=act_raw[:].rearrange("p g t -> p (g t)"))
+            bits = act_f32[:].bitcast(I32)
+            nc.vector.tensor_scalar(
+                out=mantissa[:], in0=bits, scalar1=MANTISSA_BITS, scalar2=BITS_OF_ONE,
+                op0=ALU.bitwise_and, op1=ALU.bitwise_or)
+            nc.vector.tensor_scalar(
+                out=exponent[:], in0=bits, scalar1=MANTISSA_WIDTH, scalar2=EXPONENT_MASK,
+                op0=ALU.logical_shift_right, op1=ALU.bitwise_and)
+            nc.scalar.activation(out=ln_mantissa[:], in_=mantissa[:].bitcast(F32), func=ACT.Ln)
+            nc.vector.tensor_scalar(
+                out=ln_power[:], in0=exponent[:], scalar1=EXPONENT_BIAS, scalar2=math.log(2.0),
+                op0=ALU.subtract, op1=ALU.mult)
+            nc.vector.tensor_add(out=ln_act[:], in0=ln_power[:], in1=ln_mantissa[:])
+
+        def transpose_words(bank, place, words, first):
+            nc.tensor.transpose(bank[:, place * P:(place + 1) * P], words[:, first:first + 2 * P - 1:2], identity[:])
+
+        seg_bank = {}
+        seg_grouped = {}
+
+        def turn_seg(g, h):
+            bank = new_bank()
+            seg_bank[g, h] = bank
+            for k in range(2):
+                words = seg_raw[g][h][:, k, :].bitcast(F32)
+                for u in range(2):
+                    transpose_words(bank, 2 * k + u, words, u)
+
+        def copy_seg(g, h, copy):
+            grouped = work.tile([P, 2 * P * PACK], BF16, name="seg_grouped%d" % h, align_bytes=64)
+            seg_grouped[g, h] = grouped
+            copy(
+                out=grouped[:].bitcast(F32).rearrange("p (t m u) -> p t m u", t=2, u=2),
+                in_=seg_bank[g, h][:].rearrange("p (t u m) -> p t m u", t=2, u=2))
+
+        def quantize_seg(g, h):
+            first = g * PASS + h * 2 * P
+            cols = slice(first, first + 2 * P)
+            nc.vector.quantize_mx(
+                out=seg_codes[:, cols].bitcast(FP8X4), scales=seg_scales[:, cols], in_=seg_grouped[g, h][:])
+
+        def interleave(grouped, rows):
+            nc.vector.tensor_copy(
+                out=grouped.rearrange("p (n i t) -> p n t i", i=4, t=PACK),
+                in_=rows.rearrange("p t (n i) -> p n t i", i=4))
+
+        probe_grouped = {}
+
+        def interleave_probe(c):
+            q0, w = CHUNKS[c]
+            grouped = work.tile([P, w * PACK], BF16, name="probe_grouped%d" % w, align_bytes=64)
+            probe_grouped[c] = grouped
+            load = min(c, len(PROBE_LOADS) - 1)
+            first = q0 - PROBE_LOADS[load][0]
+            interleave(grouped[:], probe_raw[load][:, :, first:first + w])
+
+        def quantize_probe(c):
+            q0, w = CHUNKS[c]
+            cols = slice(q0, q0 + w)
+            nc.vector.quantize_mx(
+                out=probe_codes[:, cols].bitcast(FP8X4), scales=probe_scales[:, cols], in_=probe_grouped[c][:])
+
+        prof_bank = {}
+        prof_grouped = {}
+
+        def turn_prof(i):
+            bank = new_bank()
+            prof_bank[i] = bank
+            words = prof_raw[i // 2][:, i % 2, :].bitcast(F32)
+            for g in range(NG):
+                for u in range(2):
+                    transpose_words(bank, 2 * g + u, words, 2 * P * g + u)
+
+        def copy_prof(i, copy):
+            if i % 2 == 0:
+                grouped = work.tile([P, 2, NG * P * PACK], BF16, name="prof_grouped", align_bytes=64)
+                prof_grouped[i // 2] = grouped
+            copy(
+                out=prof_grouped[i // 2][:, i % 2, :].bitcast(F32).rearrange("p (g r u) -> p g r u", g=NG, u=2),
+                in_=prof_bank[i][:].rearrange("p (g u r) -> p g r u", g=NG, u=2))
+
+        def quantize_prof(h):
+            cols = slice(2 * h * NG * P, 2 * (h + 1) * NG * P)
+            nc.vector.quantize_mx(
+                out=prof_codes[:, cols].bitcast(FP8X4), scales=prof_scales[:, cols],
+                in_=prof_grouped[h][:].rearrange("p i n -> p (i n)"))
+
+        b_rows = {}
+        b_grouped = {}
+
+        def make_b(c, g):
+            q0, w = CHUNKS[c]
+            rows = work.tile([P, PACK, w], BF16, name="b_rows%d_%d" % (g, w))
+            b_rows[c, g] = rows
+            q_cols = slice(q0, q0 + w)
+            for t in range(PACK):
+                s_cols = slice(g * PASS + t * P, g * PASS + (t + 1) * P)
+                bank = new_bank()
+                nc.tensor.matmul_mx(
+                    out=bank[:, 0:w],
+                    lhsT=seg_codes[:, s_cols].bitcast(FP8X4), lhsT_scale=seg_scales[:, s_cols],
+                    rhs=probe_codes[:, q_cols].bitcast(FP8X4), rhs_scale=probe_scales[:, q_cols],
+                    start=True, stop=True)
+                k = g * PACK + t
+                nc.scalar.activation(out=rows[:, t, :], in_=bank[:, 0:w], func=ACT.Exp, bias=ln_act[:, k:k + 1])
+
+        def interleave_b(c, g):
+            q0, w = CHUNKS[c]
+            if g == 0:
+                grouped = work.tile([P, NG, w * PACK], BF16, name="b_grouped%d" % w, align_bytes=64)
+                b_grouped[c] = grouped
+            interleave(b_grouped[c][:, g, :], b_rows[c, g][:])
+
+        def quantize_b(c):
+            q0, w = CHUNKS[c]
+            cols = slice(NG * q0, NG * (q0 + w))
+            nc.vector.quantize_mx(
+                out=b_codes[:, cols].bitcast(FP8X4), scales=b_scales[:, cols],
+                in_=b_grouped[c][:].rearrange("p g n -> p (g n)"))
+
+        roots = {}
+
+        def make_roots(i, bank_number, pieces=1):
+            half = bank_number * BANK // HALF
+            if (i, half) not in roots:
+                root = root_pool.tile([P, HALF], F32, name="root")
+                roots[i, half] = root
+            bank = new_bank()
+            for q0, w in CHUNKS:
+                if q0 // BANK == bank_number:
+                    place = q0 % BANK
+                    for g in range(NG):
+                        m_cols = slice((i * NG + g) * P, (i * NG + g + 1) * P)
+                        q_cols = slice(NG * q0 + g * w, NG * q0 + (g + 1) * w)
+                        nc.tensor.matmul_mx(
+                            out=bank[:, place:place + w],
+                            lhsT=prof_codes[:, m_cols].bitcast(FP8X4), lhsT_scale=prof_scales[:, m_cols],
+                            rhs=b_codes[:, q_cols].bitcast(FP8X4), rhs_scale=b_scales[:, q_cols],
+                            start=(g == 0), stop=(g == NG - 1))
+            step = BANK // pieces
+            for x in range(0, BANK, step):
+                first = bank_number * BANK - half * HALF + x
+                nc.scalar.activation(
+                    out=roots[i, half][:, first:first + step], in_=bank[:, x:x + step], func=ACT.Abs_reciprocal_sqrt)
+
+        def left_roots(i):
+            make_roots(i, 0)
+            make_roots(i, 1)
+
+        def right_roots(i):
+            make_roots(i, 2)
+            make_roots(i, 3)
+
+        def square(result, root):
+            nc.vector.tensor_mul(out=result, in0=root, in1=root)
+
+        def scalar_square(result, root):
+            nc.scalar.activation(out=result, in_=root, func=ACT.Square)
+
+        def finish(i, half, squared_by=square, first=0, width=HALF):
+            result = result_pool.tile([P, width], F32, name="result%d" % width)
+            squared_by(result[:], roots[i, half][:, first:first + width])
+            q0 = half * HALF + first
+            nc.sync.dma_start(out=out[i * P:(i + 1) * P, q0:q0 + width], in_=result[:])
+
+        by_vector = nc.vector.tensor_copy
+        by_scalar = nc.scalar.copy
+        left, right = 0, 1
+
         with tc.manual_schedule():
-            nc.scalar.dma_start(out=act_sb[:], in_=act_view)
+            nc.scalar.dma_start(out=act_raw[:], in_=act_view)
             nc.vector.memset(one[:], 1.0)
-            nc.scalar.activation(out=junk[:], in_=one[:], func=ACT.Ln)
-
-            seg_raw = [[keep.tile([P, 2, D], BF16, name="seg_raw%d_%d" % (g, h)) for h in range(2)] for g in range(NG)]
-            probe_raw = [keep.tile([P, PACK, w], BF16, name="probe_raw%d" % q0) for q0, w in LOADS]
-            prof_raw = [keep.tile([P, 2, S], BF16, name="prof_raw%d" % h) for h in range(NI // 2)]
-
-            def load_seg(g, h):
-                nc.sync.dma_start(out=seg_raw[g][h][:], in_=seg_view[g][:, 2 * h:2 * h + 2, :])
-
-            def load_probe(c):
-                q0, w = LOADS[c]
-                nc.sync.dma_start(out=probe_raw[c][:], in_=probe_view[:, :, q0:q0 + w])
-
-            def load_prof(h):
-                nc.sync.dma_start(out=prof_raw[h][:], in_=prof_view[:, 2 * h:2 * h + 2, :])
+            nc.scalar.activation(out=unused[:], in_=one[:], func=ACT.Ln)
 
             load_seg(0, 0)
             load_probe(0)
@@ -90,260 +276,99 @@ def tile_cosmo_segment_activities_s7_kernel(tc, seg, probe, act, prof, out):
             load_prof(2)
             load_prof(3)
 
-            nc.scalar.activation(out=ln_act[:], in_=act_sb[:].rearrange("p g t -> p (g t)"), func=ACT.Ln)
-            nc.scalar.activation(out=junk[:], in_=one[:], func=ACT.Exp)
+            make_ln_act()
+            nc.scalar.activation(out=unused[:], in_=one[:], func=ACT.Exp)
 
-            seg_bank = {}
-            seg_grouped = {}
+            turn_seg(0, 0)
+            copy_seg(0, 0, by_vector)
+            turn_seg(0, 1)
+            interleave_probe(0)
+            turn_seg(1, 0)
+            quantize_seg(0, 0)
+            copy_seg(0, 1, by_scalar)
+            copy_seg(1, 0, by_scalar)
+            quantize_probe(0)
+            quantize_seg(0, 1)
+            make_b(0, 0)
+            turn_seg(1, 1)
+            interleave_probe(1)
+            quantize_seg(1, 0)
+            quantize_probe(1)
+            copy_seg(1, 1, by_scalar)
+            interleave_probe(2)
+            make_b(1, 0)
+            quantize_seg(1, 1)
+            quantize_probe(2)
+            interleave_b(0, 0)
+            make_b(0, 1)
+            interleave_b(1, 0)
+            interleave_b(0, 1)
+            interleave_probe(3)
+            make_b(1, 1)
 
-            def seg_t(g, h):
-                bank = psum_bank()
-                seg_bank[g, h] = bank
-                for k in range(2):
-                    words = seg_raw[g][h][:, k, :].bitcast(F32)
-                    for u in range(2):
-                        x = 2 * k + u
-                        nc.tensor.transpose(bank[:, x * P:(x + 1) * P], words[:, u::2], ident[:])
+            turn_prof(0)
+            copy_prof(0, by_vector)
+            make_b(2, 0)
+            interleave_probe(4)
+            turn_prof(1)
+            quantize_probe(3)
+            make_b(2, 1)
+            copy_prof(1, by_vector)
+            make_b(3, 0)
+            interleave_b(1, 1)
+            quantize_probe(4)
+            interleave_b(2, 0)
+            turn_prof(2)
+            copy_prof(2, by_scalar)
+            make_b(3, 1)
+            turn_prof(3)
+            quantize_prof(0)
+            interleave_b(2, 1)
+            turn_prof(4)
+            copy_prof(3, by_vector)
+            make_b(4, 0)
+            turn_prof(5)
+            copy_prof(4, by_scalar)
+            make_b(4, 1)
+            turn_prof(6)
+            quantize_b(0)
+            quantize_b(1)
+            quantize_b(2)
+            copy_prof(5, by_vector)
+            quantize_prof(1)
+            interleave_b(3, 0)
+            turn_prof(7)
+            quantize_prof(2)
 
-            def seg_c(g, h, copy):
-                grouped = work.tile([P, 2 * P * PACK], BF16, name="seg_grouped%d" % h, align_bytes=64)
-                seg_grouped[g, h] = grouped
-                copy(
-                    out=grouped[:].bitcast(F32).rearrange("j (t p u) -> j t p u", t=2, u=2),
-                    in_=seg_bank[g, h][:].rearrange("j (t u p) -> j t p u", t=2, u=2))
+            left_roots(0)
+            left_roots(1)
+            interleave_b(3, 1)
+            interleave_b(4, 0)
+            copy_prof(6, by_vector)
+            interleave_b(4, 1)
+            left_roots(2)
+            copy_prof(7, by_vector)
+            finish(1, left, scalar_square)
+            left_roots(3)
+            finish(0, left)
+            quantize_prof(3)
+            left_roots(4)
+            finish(2, left)
+            finish(3, left, scalar_square)
+            quantize_b(3)
+            quantize_b(4)
+            for i in (5, 6, 7):
+                left_roots(i)
+                finish(i - 1, left)
 
-            def seg_q(g, h):
-                c0 = g * KP + h * 2 * P
-                cols = slice(c0, c0 + 2 * P)
-                nc.vector.quantize_mx(
-                    out=seg_codes[:, cols].bitcast(FP8X4), scales=seg_scales[:, cols], in_=seg_grouped[g, h][:])
-
-            def interleave(dst, src):
-                nc.vector.tensor_copy(
-                    out=dst.rearrange("p (c i t) -> p c t i", i=4, t=PACK),
-                    in_=src.rearrange("p t (c i) -> p c t i", i=4))
-
-            probe_grouped = {}
-
-            def p_i(c):
-                q0, w = CHUNKS[c]
-                grouped = work.tile([P, w * PACK], BF16, name="probe_grouped%d" % w, align_bytes=64)
-                probe_grouped[c] = grouped
-                k = min(c, len(LOADS) - 1)
-                first = q0 - LOADS[k][0]
-                interleave(grouped[:], probe_raw[k][:, :, first:first + w])
-
-            def p_q(c):
-                q0, w = CHUNKS[c]
-                cols = slice(q0, q0 + w)
-                nc.vector.quantize_mx(
-                    out=probe_codes[:, cols].bitcast(FP8X4), scales=probe_scales[:, cols], in_=probe_grouped[c][:])
-
-            prof_bank = {}
-            prof_grouped = {}
-
-            def prof_t(i):
-                bank = psum_bank()
-                prof_bank[i] = bank
-                words = prof_raw[i // 2][:, i % 2, :].bitcast(F32)
-                for g in range(NG):
-                    for u in range(2):
-                        x = 2 * g + u
-                        nc.tensor.transpose(
-                            bank[:, x * P:(x + 1) * P], words[:, 256 * g + u:256 * (g + 1):2], ident[:])
-
-            def prof_c(i, copy):
-                if i % 2 == 0:
-                    grouped = work.tile([P, 2, NG * P * PACK], BF16, name="prof_grouped", align_bytes=64)
-                    prof_grouped[i // 2] = grouped
-                copy(
-                    out=prof_grouped[i // 2][:, i % 2, :].bitcast(F32).rearrange("j (g r u) -> j g r u", g=NG, u=2),
-                    in_=prof_bank[i][:].rearrange("j (g u r) -> j g r u", g=NG, u=2))
-
-            def prof_q(h):
-                cols = slice(2 * h * NG * P, 2 * (h + 1) * NG * P)
-                nc.vector.quantize_mx(
-                    out=prof_codes[:, cols].bitcast(FP8X4), scales=prof_scales[:, cols],
-                    in_=prof_grouped[h][:].rearrange("p i n -> p (i n)"))
-
-            b_parts = {}
-
-            def e(c, g, t):
-                q0, w = CHUNKS[c]
-                if (c, g) not in b_parts:
-                    parts = work.tile([P, PACK, w], BF16, name="b_parts%d_%d" % (g, w))
-                    b_parts[c, g] = parts
-                cols = slice(q0, q0 + w)
-                s_cols = slice(g * KP + t * P, g * KP + (t + 1) * P)
-                bank = psum_bank()
-                nc.tensor.matmul_mx(
-                    out=bank[:, 0:w],
-                    lhsT=seg_codes[:, s_cols].bitcast(FP8X4), lhsT_scale=seg_scales[:, s_cols],
-                    rhs=probe_codes[:, cols].bitcast(FP8X4), rhs_scale=probe_scales[:, cols],
-                    start=True, stop=True)
-                k = g * PACK + t
-                nc.scalar.activation(
-                    out=b_parts[c, g][:, t, :], in_=bank[:, 0:w], func=ACT.Exp, bias=ln_act[:, k:k + 1])
-
-            b_grouped = {}
-
-            def b_i(c, g):
-                q0, w = CHUNKS[c]
-                if g == 0:
-                    grouped = work.tile([P, NG, w * PACK], BF16, name="b_grouped%d" % w, align_bytes=64)
-                    b_grouped[c] = grouped
-                interleave(b_grouped[c][:, g, :], b_parts[c, g][:])
-
-            def b_q(c):
-                q0, w = CHUNKS[c]
-                cols = slice(NG * q0, NG * (q0 + w))
-                nc.vector.quantize_mx(
-                    out=b_codes[:, cols].bitcast(FP8X4), scales=b_scales[:, cols],
-                    in_=b_grouped[c][:].rearrange("p g n -> p (g n)"))
-
-            roots = {}
-
-            def z(i, n, pieces=1):
-                half = n // 2
-                if (i, half) not in roots:
-                    root = outp.tile([P, 2 * BANK], F32, name="root")
-                    roots[i, half] = root
-                bank = psum_bank()
-                for q0, w in CHUNKS:
-                    if q0 // BANK == n:
-                        for g in range(NG):
-                            s_cols = slice((i * NG + g) * P, (i * NG + g + 1) * P)
-                            cols = slice(NG * q0 + g * w, NG * q0 + (g + 1) * w)
-                            nc.tensor.matmul_mx(
-                                out=bank[:, q0 % BANK:q0 % BANK + w],
-                                lhsT=prof_codes[:, s_cols].bitcast(FP8X4), lhsT_scale=prof_scales[:, s_cols],
-                                rhs=b_codes[:, cols].bitcast(FP8X4), rhs_scale=b_scales[:, cols],
-                                start=(g == 0), stop=(g == NG - 1))
-                step = BANK // pieces
-                for x in range(0, BANK, step):
-                    r0 = (n % 2) * BANK + x
-                    nc.scalar.activation(
-                        out=roots[i, half][:, r0:r0 + step], in_=bank[:, x:x + step], func=ACT.Abs_reciprocal_sqrt)
-
-            def sq(i, half, r0, w, scalar=0):
-                result = store.tile([P, w], F32, name="result%d" % w)
-                root = roots[i, half][:, r0:r0 + w]
-                if scalar:
-                    nc.scalar.activation(out=result[:], in_=root, func=ACT.Square)
-                else:
-                    nc.vector.tensor_mul(out=result[:], in0=root, in1=root)
-                q0 = half * 2 * BANK + r0
-                nc.sync.dma_start(out=out[i * P:(i + 1) * P, q0:q0 + w], in_=result[:])
-
-            def E(c, g, ts=range(PACK)):
-                for t in ts:
-                    e(c, g, t)
-
-            def Z(i, half, pieces=1):
-                z(i, 2 * half)
-                z(i, 2 * half + 1, pieces)
-
-            V = nc.vector.tensor_copy
-            A = nc.scalar.copy
-            p_i(0)
-            seg_t(0, 0)
-            seg_t(0, 1)
-            seg_t(1, 0)
-            seg_c(0, 0, V)
-            p_q(0)
-            seg_q(0, 0)
-            seg_c(0, 1, A)
-            seg_c(1, 0, A)
-            seg_q(0, 1)
-            p_i(1)
-            E(0, 0)
-            seg_q(1, 0)
-            seg_t(1, 1)
-            seg_c(1, 1, A)
-            p_q(1)
-            p_i(2)
-            seg_q(1, 1)
-            b_i(0, 0)
-            E(1, 0)
-            b_i(1, 0)
-            p_q(2)
-            E(1, 1)
-            E(0, 1)
-            b_i(1, 1)
-            b_i(0, 1)
-            E(2, 0)
-            prof_t(0)
-            E(2, 1)
-            p_i(3)
-            p_i(4)
-            p_q(3)
-            prof_c(0, V)
-            prof_t(1)
-            p_q(4)
-            b_i(2, 0)
-            prof_c(1, A)
-            b_i(2, 1)
-            E(3, 0)
-            E(4, 0)
-            prof_t(2)
-            prof_t(3)
-            E(3, 1)
-            prof_c(2, V)
-            prof_c(3, V)
-            prof_q(0)
-            E(4, 1)
-            prof_t(4)
-            prof_t(5)
-            b_q(0)
-            b_q(2)
-            prof_q(1)
-            b_q(1)
-            b_i(4, 0)
-            Z(0, 0)
-            prof_c(4, V)
-            Z(1, 0)
-            prof_t(6)
-            prof_t(7)
-            b_i(3, 0)
-            prof_c(6, V)
-            b_i(3, 1)
-            prof_c(5, V)
-            sq(0, 0, 0, 1024)
-            Z(2, 0)
-            prof_q(2)
-            sq(1, 0, 0, 1024, 1)
-            prof_c(7, A)
-            sq(2, 0, 0, 1024)
-            b_i(4, 1)
-            prof_q(3)
-            b_q(4)
-            Z(3, 0)
-            Z(4, 0)
-            sq(3, 0, 0, 1024, 1)
-            Z(5, 0)
-            Z(6, 0)
-            b_q(3)
-            sq(4, 0, 0, 1024)
-            Z(7, 0)
-            sq(5, 0, 0, 1024)
-            Z(0, 1)
-            sq(6, 0, 0, 1024)
-            Z(1, 1)
-            sq(7, 0, 0, 1024)
-            Z(2, 1)
-            sq(0, 1, 0, 1024)
-            Z(3, 1)
-            sq(1, 1, 0, 1024)
-            Z(4, 1)
-            sq(2, 1, 0, 1024)
-            Z(5, 1)
-            sq(3, 1, 0, 1024)
-            Z(6, 1)
-            sq(4, 1, 0, 1024)
-            z(7, 2)
-            z(7, 3, 2)
-            sq(5, 1, 0, 1024)
-            sq(7, 1, 0, 512)
-            sq(7, 1, 512, 256, 1)
-            sq(7, 1, 768, 256, 1)
-            sq(6, 1, 0, 1024, 1)
+            right_roots(0)
+            finish(7, left)
+            for i in range(1, NI - 1):
+                right_roots(i)
+                finish(i - 1, right)
+            make_roots(NI - 1, 2)
+            finish(NI - 2, right)
+            make_roots(NI - 1, 3, pieces=2)
+            finish(NI - 1, right, first=0, width=BANK)
+            finish(NI - 1, right, first=BANK, width=BANK // 2)
+            finish(NI - 1, right, first=BANK + BANK // 2, width=BANK // 2)

import math
from contextlib import ExitStack

import concourse.mybir as mybir
from concourse.masks import make_identity

M, S, Q, D = 1024, 1024, 2048, 512
FLOPS = 2 * S * D * Q + 2 * M * S * Q

F32 = mybir.dt.float32
BF16 = mybir.dt.bfloat16
I32 = mybir.dt.int32
U32 = mybir.dt.uint32
U8 = mybir.dt.uint8
FP8X4 = mybir.dt.float8_e4m3fn_x4
ACT = mybir.ActivationFunctionType
ALU = mybir.AluOpType

P = 128
PACK = 4
PASS = P * PACK
BANK = 512
NG = S // PASS
NI = M // P
HALF = Q // 2

CHUNKS = ((0, 256), (256, 256), (512, 512), (1024, 512), (1536, 512))
PROBE_LOADS = ((0, 256), (256, 256), (512, 512), (1024, 1024))

MANTISSA_BITS = 0x007FFFFF
BITS_OF_ONE = 0x3F800000
MANTISSA_WIDTH = 23
EXPONENT_MASK = 0xFF
EXPONENT_BIAS = 127.0


def tile_cosmo_segment_activities_s7_kernel(tc, seg, probe, act, prof, out):
    nc = tc.nc
    with ExitStack() as ctx:
        keep = ctx.enter_context(tc.tile_pool(name="keep", bufs=1))
        work = ctx.enter_context(tc.tile_pool(name="work", bufs=2))
        root_pool = ctx.enter_context(tc.tile_pool(name="root_pool", bufs=4))
        result_pool = ctx.enter_context(tc.tile_pool(name="result_pool", bufs=6))
        psum = ctx.enter_context(tc.psum_pool(name="psum", bufs=8))

        seg_view = seg.rearrange("(g p t) d -> g p t d", g=NG, t=PACK)
        probe_view = probe.rearrange("(p t) q -> p t q", t=PACK)
        prof_view = prof.rearrange("(i r) s -> r i s", r=P)
        act_view = act.rearrange("(g p t) -> p g t", g=NG, t=PACK)

        identity = keep.tile([P, P], F32, name="identity")
        make_identity(nc, identity[:])

        seg_codes = keep.tile([P, S], U32, name="seg_codes", align_bytes=64)
        seg_scales = keep.tile([P, S], U8, name="seg_scales", align_bytes=64)
        probe_codes = keep.tile([P, Q], U32, name="probe_codes", align_bytes=64)
        probe_scales = keep.tile([P, Q], U8, name="probe_scales", align_bytes=64)
        prof_codes = keep.tile([P, NI * NG * P], U32, name="prof_codes", align_bytes=64)
        prof_scales = keep.tile([P, NI * NG * P], U8, name="prof_scales", align_bytes=64)
        b_codes = keep.tile([P, NG * Q], U32, name="b_codes", align_bytes=64)
        b_scales = keep.tile([P, NG * Q], U8, name="b_scales", align_bytes=64)

        seg_raw = [[keep.tile([P, 2, D], BF16, name="seg_raw%d_%d" % (g, h)) for h in range(2)] for g in range(NG)]
        probe_raw = [keep.tile([P, PACK, w], BF16, name="probe_raw%d" % q0) for q0, w in PROBE_LOADS]
        prof_raw = [keep.tile([P, 2, S], BF16, name="prof_raw%d" % h) for h in range(NI // 2)]

        act_raw = keep.tile([P, NG, PACK], BF16, name="act_raw")
        act_f32 = keep.tile([P, NG * PACK], F32, name="act_f32")
        mantissa = keep.tile([P, NG * PACK], I32, name="mantissa")
        exponent = keep.tile([P, NG * PACK], I32, name="exponent")
        ln_mantissa = keep.tile([P, NG * PACK], F32, name="ln_mantissa")
        ln_power = keep.tile([P, NG * PACK], F32, name="ln_power")
        ln_act = keep.tile([P, NG * PACK], F32, name="ln_act")
        one = keep.tile([P, 1], F32, name="one")
        unused = keep.tile([P, 1], F32, name="unused")

        def new_bank():
            bank = psum.tile([P, BANK], F32, name="bank")
            return bank

        def load_seg(g, h):
            nc.sync.dma_start(out=seg_raw[g][h][:], in_=seg_view[g][:, 2 * h:2 * h + 2, :])

        def load_probe(n):
            q0, w = PROBE_LOADS[n]
            nc.sync.dma_start(out=probe_raw[n][:], in_=probe_view[:, :, q0:q0 + w])

        def load_prof(h):
            nc.sync.dma_start(out=prof_raw[h][:], in_=prof_view[:, 2 * h:2 * h + 2, :])

        def make_ln_act():
            nc.vector.tensor_copy(out=act_f32[:], in_=act_raw[:].rearrange("p g t -> p (g t)"))
            bits = act_f32[:].bitcast(I32)
            nc.vector.tensor_scalar(
                out=mantissa[:], in0=bits, scalar1=MANTISSA_BITS, scalar2=BITS_OF_ONE,
                op0=ALU.bitwise_and, op1=ALU.bitwise_or)
            nc.vector.tensor_scalar(
                out=exponent[:], in0=bits, scalar1=MANTISSA_WIDTH, scalar2=EXPONENT_MASK,
                op0=ALU.logical_shift_right, op1=ALU.bitwise_and)
            nc.scalar.activation(out=ln_mantissa[:], in_=mantissa[:].bitcast(F32), func=ACT.Ln)
            nc.vector.tensor_scalar(
                out=ln_power[:], in0=exponent[:], scalar1=EXPONENT_BIAS, scalar2=math.log(2.0),
                op0=ALU.subtract, op1=ALU.mult)
            nc.vector.tensor_add(out=ln_act[:], in0=ln_power[:], in1=ln_mantissa[:])

        def transpose_words(bank, place, words, first):
            nc.tensor.transpose(bank[:, place * P:(place + 1) * P], words[:, first:first + 2 * P - 1:2], identity[:])

        seg_bank = {}
        seg_grouped = {}

        def turn_seg(g, h):
            bank = new_bank()
            seg_bank[g, h] = bank
            for k in range(2):
                words = seg_raw[g][h][:, k, :].bitcast(F32)
                for u in range(2):
                    transpose_words(bank, 2 * k + u, words, u)

        def copy_seg(g, h, copy):
            grouped = work.tile([P, 2 * P * PACK], BF16, name="seg_grouped%d" % h, align_bytes=64)
            seg_grouped[g, h] = grouped
            copy(
                out=grouped[:].bitcast(F32).rearrange("p (t m u) -> p t m u", t=2, u=2),
                in_=seg_bank[g, h][:].rearrange("p (t u m) -> p t m u", t=2, u=2))

        def quantize_seg(g, h):
            first = g * PASS + h * 2 * P
            cols = slice(first, first + 2 * P)
            nc.vector.quantize_mx(
                out=seg_codes[:, cols].bitcast(FP8X4), scales=seg_scales[:, cols], in_=seg_grouped[g, h][:])

        def interleave(grouped, rows):
            nc.vector.tensor_copy(
                out=grouped.rearrange("p (n i t) -> p n t i", i=4, t=PACK),
                in_=rows.rearrange("p t (n i) -> p n t i", i=4))

        probe_grouped = {}

        def interleave_probe(c):
            q0, w = CHUNKS[c]
            grouped = work.tile([P, w * PACK], BF16, name="probe_grouped%d" % w, align_bytes=64)
            probe_grouped[c] = grouped
            load = min(c, len(PROBE_LOADS) - 1)
            first = q0 - PROBE_LOADS[load][0]
            interleave(grouped[:], probe_raw[load][:, :, first:first + w])

        def quantize_probe(c):
            q0, w = CHUNKS[c]
            cols = slice(q0, q0 + w)
            nc.vector.quantize_mx(
                out=probe_codes[:, cols].bitcast(FP8X4), scales=probe_scales[:, cols], in_=probe_grouped[c][:])

        prof_bank = {}
        prof_grouped = {}

        def turn_prof(i):
            bank = new_bank()
            prof_bank[i] = bank
            words = prof_raw[i // 2][:, i % 2, :].bitcast(F32)
            for g in range(NG):
                for u in range(2):
                    transpose_words(bank, 2 * g + u, words, 2 * P * g + u)

        def copy_prof(i, copy):
            if i % 2 == 0:
                grouped = work.tile([P, 2, NG * P * PACK], BF16, name="prof_grouped", align_bytes=64)
                prof_grouped[i // 2] = grouped
            copy(
                out=prof_grouped[i // 2][:, i % 2, :].bitcast(F32).rearrange("p (g r u) -> p g r u", g=NG, u=2),
                in_=prof_bank[i][:].rearrange("p (g u r) -> p g r u", g=NG, u=2))

        def quantize_prof(h):
            cols = slice(2 * h * NG * P, 2 * (h + 1) * NG * P)
            nc.vector.quantize_mx(
                out=prof_codes[:, cols].bitcast(FP8X4), scales=prof_scales[:, cols],
                in_=prof_grouped[h][:].rearrange("p i n -> p (i n)"))

        b_rows = {}
        b_grouped = {}

        def make_b(c, g):
            q0, w = CHUNKS[c]
            rows = work.tile([P, PACK, w], BF16, name="b_rows%d_%d" % (g, w))
            b_rows[c, g] = rows
            q_cols = slice(q0, q0 + w)
            for t in range(PACK):
                s_cols = slice(g * PASS + t * P, g * PASS + (t + 1) * P)
                bank = new_bank()
                nc.tensor.matmul_mx(
                    out=bank[:, 0:w],
                    lhsT=seg_codes[:, s_cols].bitcast(FP8X4), lhsT_scale=seg_scales[:, s_cols],
                    rhs=probe_codes[:, q_cols].bitcast(FP8X4), rhs_scale=probe_scales[:, q_cols],
                    start=True, stop=True)
                k = g * PACK + t
                nc.scalar.activation(out=rows[:, t, :], in_=bank[:, 0:w], func=ACT.Exp, bias=ln_act[:, k:k + 1])

        def interleave_b(c, g):
            q0, w = CHUNKS[c]
            if g == 0:
                grouped = work.tile([P, NG, w * PACK], BF16, name="b_grouped%d" % w, align_bytes=64)
                b_grouped[c] = grouped
            interleave(b_grouped[c][:, g, :], b_rows[c, g][:])

        def quantize_b(c):
            q0, w = CHUNKS[c]
            cols = slice(NG * q0, NG * (q0 + w))
            nc.vector.quantize_mx(
                out=b_codes[:, cols].bitcast(FP8X4), scales=b_scales[:, cols],
                in_=b_grouped[c][:].rearrange("p g n -> p (g n)"))

        roots = {}

        def make_roots(i, bank_number, pieces=1):
            half = bank_number * BANK // HALF
            if (i, half) not in roots:
                root = root_pool.tile([P, HALF], F32, name="root")
                roots[i, half] = root
            bank = new_bank()
            for q0, w in CHUNKS:
                if q0 // BANK == bank_number:
                    place = q0 % BANK
                    for g in range(NG):
                        m_cols = slice((i * NG + g) * P, (i * NG + g + 1) * P)
                        q_cols = slice(NG * q0 + g * w, NG * q0 + (g + 1) * w)
                        nc.tensor.matmul_mx(
                            out=bank[:, place:place + w],
                            lhsT=prof_codes[:, m_cols].bitcast(FP8X4), lhsT_scale=prof_scales[:, m_cols],
                            rhs=b_codes[:, q_cols].bitcast(FP8X4), rhs_scale=b_scales[:, q_cols],
                            start=(g == 0), stop=(g == NG - 1))
            step = BANK // pieces
            for x in range(0, BANK, step):
                first = bank_number * BANK - half * HALF + x
                nc.scalar.activation(
                    out=roots[i, half][:, first:first + step], in_=bank[:, x:x + step], func=ACT.Abs_reciprocal_sqrt)

        def left_roots(i):
            make_roots(i, 0)
            make_roots(i, 1)

        def right_roots(i):
            make_roots(i, 2)
            make_roots(i, 3)

        def square(result, root):
            nc.vector.tensor_mul(out=result, in0=root, in1=root)

        def scalar_square(result, root):
            nc.scalar.activation(out=result, in_=root, func=ACT.Square)

        def finish(i, half, squared_by=square, first=0, width=HALF):
            result = result_pool.tile([P, width], F32, name="result%d" % width)
            squared_by(result[:], roots[i, half][:, first:first + width])
            q0 = half * HALF + first
            nc.sync.dma_start(out=out[i * P:(i + 1) * P, q0:q0 + width], in_=result[:])

        by_vector = nc.vector.tensor_copy
        by_scalar = nc.scalar.copy
        left, right = 0, 1

        with tc.manual_schedule():
            nc.scalar.dma_start(out=act_raw[:], in_=act_view)
            nc.vector.memset(one[:], 1.0)
            nc.scalar.activation(out=unused[:], in_=one[:], func=ACT.Ln)

            load_seg(0, 0)
            load_probe(0)
            load_seg(0, 1)
            load_seg(1, 0)
            load_probe(1)
            load_seg(1, 1)
            load_probe(2)
            load_prof(0)
            load_probe(3)
            load_prof(1)
            load_prof(2)
            load_prof(3)

            make_ln_act()
            nc.scalar.activation(out=unused[:], in_=one[:], func=ACT.Exp)

            turn_seg(0, 0)
            copy_seg(0, 0, by_vector)
            turn_seg(0, 1)
            interleave_probe(0)
            turn_seg(1, 0)
            quantize_seg(0, 0)
            copy_seg(0, 1, by_scalar)
            copy_seg(1, 0, by_scalar)
            quantize_probe(0)
            quantize_seg(0, 1)
            make_b(0, 0)
            turn_seg(1, 1)
            interleave_probe(1)
            quantize_seg(1, 0)
            quantize_probe(1)
            copy_seg(1, 1, by_scalar)
            interleave_probe(2)
            make_b(1, 0)
            quantize_seg(1, 1)
            quantize_probe(2)
            interleave_b(0, 0)
            make_b(0, 1)
            interleave_b(1, 0)
            interleave_b(0, 1)
            interleave_probe(3)
            make_b(1, 1)

            turn_prof(0)
            copy_prof(0, by_vector)
            make_b(2, 0)
            interleave_probe(4)
            turn_prof(1)
            quantize_probe(3)
            make_b(2, 1)
            copy_prof(1, by_vector)
            make_b(3, 0)
            interleave_b(1, 1)
            quantize_probe(4)
            interleave_b(2, 0)
            turn_prof(2)
            copy_prof(2, by_scalar)
            make_b(3, 1)
            turn_prof(3)
            quantize_prof(0)
            interleave_b(2, 1)
            turn_prof(4)
            copy_prof(3, by_vector)
            make_b(4, 0)
            turn_prof(5)
            copy_prof(4, by_scalar)
            make_b(4, 1)
            turn_prof(6)
            quantize_b(0)
            quantize_b(1)
            quantize_b(2)
            copy_prof(5, by_vector)
            quantize_prof(1)
            interleave_b(3, 0)
            turn_prof(7)
            quantize_prof(2)

            left_roots(0)
            left_roots(1)
            interleave_b(3, 1)
            interleave_b(4, 0)
            copy_prof(6, by_vector)
            interleave_b(4, 1)
            left_roots(2)
            copy_prof(7, by_vector)
            finish(1, left, scalar_square)
            left_roots(3)
            finish(0, left)
            quantize_prof(3)
            left_roots(4)
            finish(2, left)
            finish(3, left, scalar_square)
            quantize_b(3)
            quantize_b(4)
            for i in (5, 6, 7):
                left_roots(i)
                finish(i - 1, left)

            right_roots(0)
            finish(7, left)
            for i in range(1, NI - 1):
                right_roots(i)
                finish(i - 1, right)
            make_roots(NI - 1, 2)
            finish(NI - 2, right)
            make_roots(NI - 1, 3, pieces=2)
            finish(NI - 1, right, first=0, width=BANK)
            finish(NI - 1, right, first=BANK, width=BANK // 2)
            finish(NI - 1, right, first=BANK + BANK // 2, width=BANK // 2)
